import numpy as np, ml_dtypes
CORES = [15,47,79,175,207]
N = 5
NB, TK, FT = 16, 128, 1
def setup_inputs(rng):
    return {"x": rng.standard_normal((N, NB, 128, TK), dtype=np.float32).astype(ml_dtypes.bfloat16), "w1": (rng.standard_normal((N, 128, FT * 128), dtype=np.float32) / 8).astype(ml_dtypes.bfloat16), "w2": (rng.standard_normal((N, 128, FT * 128), dtype=np.float32) / np.float32(8 * np.sqrt(FT))).astype(ml_dtypes.bfloat16)}
def setup_inputs_big(rng):
    d = setup_inputs(rng)
    for k in ("x",): d[k] = (d[k].astype(np.float32) * 1048576.0).astype(d[k].dtype)
    return d
def setup_inputs_small(rng):
    d = setup_inputs(rng)
    for k in ("x",): d[k] = (d[k].astype(np.float32) * (1 / 1048576.0)).astype(d[k].dtype)
    return d
def reference(x, w1, w2):
    W1, W2 = w1.astype(np.float64), w2.astype(np.float64)
    a = x[0].astype(np.float64)
    for s in range(N):
        a = sum(np.einsum("kf,bkn->bfn", W2[s][:, 128 * f:128 * f + 128], np.maximum(np.einsum("kf,bkn->bfn", W1[s][:, 128 * f:128 * f + 128], a), 0.0)) for f in range(FT))
    y = np.full(x.shape, np.nan, ml_dtypes.bfloat16)
    y[N - 1] = a.astype(ml_dtypes.bfloat16)
    return {"y": y}

@@ -1,0 +1,203 @@
+from concourse.bass import DstId, RemoteDMATransfer
+from concourse.mybir import dt, AluOpType
+
+NB, BK, NCORES = 16, 128, 256
+
+SCRATCH = {
+    "h": ("sbuf", [128, NB * BK], "bfloat16"),
+    "wb": ("sbuf", [128, 10 * BK], "bfloat16"),
+    "wt": ("sbuf", [128, 3 * BK], "bfloat16"),
+    "cs": ("sbuf", [128, 3 * BK], "bfloat16"),
+    "idn": ("sbuf", [128, BK], "bfloat16"),
+    "z": ("sbuf", [128, BK + 1], "bfloat16"),
+    "zr": ("sbuf", [128, BK], "float32"),
+    "idd": ("dram", [BK + 1, 128], "bfloat16"),
+}
+for _b in range(8):
+    SCRATCH["ps%d" % _b] = ("psum", [128, 512], "float32")
+
+SEMAPHORES = (["wl", "zr", "idm", "id1", "id2", "ls", "st", "yr0", "yr1"]
+              + ["wa%d" % s for s in range(1, 5)] + ["pp%d" % s for s in range(1, 4)]
+              + ["xl%d" % m for m in range(NB)] + ["ch%d" % m for m in range(NB)] + ["ar%d" % w for w in range(8)])
+
+ROUNDS = [[("H", [0, 1]), ("D", [6, 7])], [("H", [2, 3]), ("D", [8, 9])], [("H", [4, 5]), ("D", [10, 11])],
+          [("D", [12, 13])], [("D", [14, 15])]]
+GROUPS = {"H": [[0, 1], [2]], "D": [[0, 1], [2, 3], [4]]}
+
+
+def _count(mask):
+    return sum((mask >> i) & 1 for i in range(32))
+
+
+def rank_program(g, core, T, topo):
+    cores = T.cores
+    src, dst = cores[0], cores[-1]
+    hlp = [c for c in range(NCORES) if c != src and topo.host(c) == topo.host(src) and topo.chip(c) == topo.chip(src)
+           and topo.die(c) == topo.die(src) and topo.may_write(c, dst)][0]
+    who = {"H": hlp, "D": dst}
+    rank = T.rank_of(core)
+    if rank is None and core != hlp:
+        return
+    off = topo.mask(src, dst)
+    on = topo.mask(src, hlp) & ~off
+    eng = {"H": on, "D": off}
+
+    seen, fin = {}, {}
+
+    def wait(q, qn, name, val):
+        if seen.get((qn, name), 0) >= val:
+            return
+        seen[(qn, name)] = val
+        q.wait_ge(T.sem[name], val)
+
+    def exp(name, n):
+        fin[name] = fin.get(name, 0) + n
+
+    def col(m, n=1):
+        return slice(m * BK, (m + n) * BK)
+
+    def did(d):
+        rid, pid = topo.addr(d, core)
+        return DstId(rid=rid, pnc=pid)
+
+    bank = {"i": 0, "free": [None] * 8}
+
+    def mm(name, cnt, lhsT, rhs, out, relu, deps):
+        b = bank["i"] % 8
+        bank["i"] += 1
+        if bank["free"][b] is not None:
+            wait(g.tensor, "t", bank["free"][b][0], bank["free"][b][1])
+        for d in deps:
+            wait(g.tensor, "t", d[0], d[1])
+        if cnt:
+            wait(g.tensor, "t", name, cnt)
+        ps = T["ps%d" % b][:, 0:BK]
+        g.tensor.matmul(ps, lhsT, rhs, True, True).then_inc(T.sem[name], 1)
+        for d in deps:
+            wait(g.vector, "v", d[0], d[1])
+        wait(g.vector, "v", name, cnt + 1)
+        if relu:
+            wait(g.vector, "v", "zr", 1)
+            g.vector.tensor_tensor(out, ps, T.zr[:], AluOpType.max).then_inc(T.sem[name], 1)
+        else:
+            g.vector.tensor_copy(out, ps).then_inc(T.sem[name], 1)
+        bank["free"][b] = (name, cnt + 2)
+        exp(name, 2)
+
+    if rank is not None:
+        g.sync.dma_start(T.wb[:, col(2 * rank)], T.w1[:]).then_inc(T.sem.wl, 16)
+        g.scalar.dma_start(T.wb[:, col(2 * rank + 1)], T.w2[:]).then_inc(T.sem.wl, 16)
+        exp("wl", 32)
+
+    if core == src or core == hlp or core == dst:
+        g.vector.memset(T.zr[:], 0.0).then_inc(T.sem.zr, 1)
+        exp("zr", 1)
+
+    def wmask(s):
+        m = ~0
+        for d in (hlp, dst):
+            if d != cores[s]:
+                m &= topo.mask(cores[s], d)
+        return m
+
+    if rank is not None and rank >= 1:
+        ds = [d for d in (hlp, dst) if d != core]
+        ap = T.wb[:, col(2 * rank, 2)]
+        wait(g, "g", "wl", 32)
+        g.remote_dma_fused([RemoteDMATransfer(dst_ids=[did(d) for d in ds], dma_engine_mask=wmask(rank),
+                                              remote_sem=T.sem["wa%d" % rank], srcs=[ap], dsts=[ap for d in ds])],
+                           local_sem=T.sem.ls)
+        exp("ls", _count(wmask(rank)))
+
+    if core == src:
+        qs, i = [g.sync, g.scalar], 0
+        for rnd in ROUNDS:
+            for _, ms in rnd:
+                for m in ms:
+                    qs[i % 2].dma_start(T.h[:, col(m)], T.x[m]).then_inc(T.sem["xl%d" % m], 16)
+                    exp("xl%d" % m, 16)
+                    i += 1
+        w = 0
+        for rnd in ROUNDS:
+            ms = [m for _, bl in rnd for m in bl]
+            for sub in range(2):
+                for m in ms:
+                    mm("ch%d" % m, 2 * sub, T.wb[:, col(sub)], T.h[:, col(m)], T.h[:, col(m)], sub == 0,
+                       [("wl", 32), ("xl%d" % m, 16)])
+            for m in ms:
+                wait(g, "g", "ch%d" % m, 4)
+            trs = []
+            for k, bl in rnd:
+                ap = T.h[:, col(bl[0], len(bl))]
+                trs.append(RemoteDMATransfer(dst_ids=[did(who[k])], dma_engine_mask=eng[k],
+                                             remote_sem=T.sem["ar%d" % w], src=ap, dst=ap))
+                exp("ls", _count(eng[k]))
+                w += 1
+            g.remote_dma_fused(trs, local_sem=T.sem.ls)
+
+    if core == hlp or core == dst:
+        me = "H" if core == hlp else "D"
+        g.vector.memset(T.z[:], 0.0).then_inc(T.sem.idm, 1)
+        wait(g.vector, "v", "idm", 1)
+        g.vector.memset(T.z[:, 0:1], 1.0).then_inc(T.sem.idm, 1)
+        wait(g.sync, "s", "idm", 2)
+        g.sync.dma_start(T.idd[:], T.z[:]).then_inc(T.sem.id1, 16)
+        wait(g.sync, "s", "id1", 16)
+        g.sync.dma_start(T.idn[:], T.idd[0:128, :]).then_inc(T.sem.id2, 16)
+        exp("idm", 2)
+        exp("id1", 16)
+        exp("id2", 16)
+
+        def wdep(s):
+            return ("wl", 32) if cores[s] == core else ("wa%d" % s, _count(wmask(s)))
+
+        for s in range(1, 5):
+            if cores[s] != core:
+                exp("wa%d" % s, _count(wmask(s)))
+        for s in range(1, 4):
+            mm("pp%d" % s, 0, T.wb[:, col(2 * s + 1)], T.idn[:], T.wt[:, col(s - 1)], False, [("id2", 16), wdep(s)])
+        for s in range(1, 4):
+            mm("pp%d" % s, 2, T.wt[:, col(s - 1)], T.wb[:, col(2 * s + 2)], T.cs[:, col(s - 1)], False, [wdep(s + 1)])
+        lhs = [(T.wb[:, col(2)], wdep(1))] + [(T.cs[:, col(s - 1)], ("pp%d" % s, 4)) for s in range(1, 4)] \
+            + [(T.wb[:, col(9)], wdep(4))]
+
+        mine, w = [], 0
+        for rnd in ROUNDS:
+            for k, bl in rnd:
+                if k == me:
+                    mine.append((w, bl))
+                    exp("ar%d" % w, _count(eng[k]))
+                w += 1
+        for gi, grp in enumerate(GROUPS[me]):
+            wm = [(mine[j][0], m) for j in grp for m in mine[j][1]]
+            for st in range(5):
+                for wv, m in wm:
+                    mm("ch%d" % m, 2 * st, lhs[st][0], T.h[:, col(m)], T.h[:, col(m)], st < 4,
+                       [lhs[st][1], ("ar%d" % wv, _count(eng[me]))])
+            if me == "H":
+                for _, m in wm:
+                    wait(g, "g", "ch%d" % m, 10)
+                ap = T.h[:, col(wm[0][1], len(wm))]
+                rid, pid = topo.addr(dst, core)
+                mk = topo.mask(core, dst)
+                g.remote_dma(ap, ap, T.sem["yr%d" % gi], T.sem.ls, pid, rid, mk)
+                exp("ls", _count(mk))
+            else:
+                for _, m in wm:
+                    wait(g.sync, "s", "ch%d" % m, 10)
+                    g.sync.dma_start(T.y[m], T.h[:, col(m)]).then_inc(T.sem.st, 16)
+                    exp("st", 16)
+
+    if core == dst:
+        hw = [bl for rnd in ROUNDS for k, bl in rnd if k == "H"]
+        for gi, grp in enumerate(GROUPS["H"]):
+            n = _count(topo.mask(hlp, dst))
+            exp("yr%d" % gi, n)
+            wait(g.scalar, "a", "yr%d" % gi, n)
+            for j in grp:
+                for m in hw[j]:
+                    g.scalar.dma_start(T.y[m], T.h[:, col(m)]).then_inc(T.sem.st, 16)
+                    exp("st", 16)
+
+    for name in fin:
+        wait(g, "g", name, fin[name])

@@ -1,7 +1,7 @@
 from concourse.bass import DstId, RemoteDMATransfer
 from concourse.mybir import dt, AluOpType
 
-NB, BK, NCORES = 16, 128, 256
+NB, BK = 16, 128
 
 SCRATCH = {
     "h": ("sbuf", [128, NB * BK], "bfloat16"),
@@ -9,20 +9,18 @@ SCRATCH = {
     "wt": ("sbuf", [128, 3 * BK], "bfloat16"),
     "cs": ("sbuf", [128, 3 * BK], "bfloat16"),
     "idn": ("sbuf", [128, BK], "bfloat16"),
-    "z": ("sbuf", [128, BK + 1], "bfloat16"),
+    "one": ("sbuf", [128, BK], "bfloat16"),
     "zr": ("sbuf", [128, BK], "float32"),
-    "idd": ("dram", [BK + 1, 128], "bfloat16"),
 }
 for _b in range(8):
     SCRATCH["ps%d" % _b] = ("psum", [128, 512], "float32")
 
-SEMAPHORES = (["wl", "zr", "idm", "id1", "id2", "ls", "st", "yr0", "yr1"]
+SEMAPHORES = (["wl", "zr", "on1", "idn", "ls", "st", "yr0"]
               + ["wa%d" % s for s in range(1, 5)] + ["pp%d" % s for s in range(1, 4)]
-              + ["xl%d" % m for m in range(NB)] + ["ch%d" % m for m in range(NB)] + ["ar%d" % w for w in range(8)])
+              + ["xl%d" % m for m in range(NB)] + ["ch%d" % m for m in range(NB)]
+              + ["ar%d" % w for w in range(3)])
 
-ROUNDS = [[("H", [0, 1]), ("D", [6, 7])], [("H", [2, 3]), ("D", [8, 9])], [("H", [4, 5]), ("D", [10, 11])],
-          [("D", [12, 13])], [("D", [14, 15])]]
-GROUPS = {"H": [[0, 1], [2]], "D": [[0, 1], [2, 3], [4]]}
+WAVES = [("D", [0, 1, 2, 3, 4, 5]), ("D", [6, 7, 8, 9]), ("S", [10, 11, 12, 13, 14, 15])]
 
 
 def _count(mask):
@@ -32,15 +30,10 @@ def _count(mask):
 def rank_program(g, core, T, topo):
     cores = T.cores
     src, dst = cores[0], cores[-1]
-    hlp = [c for c in range(NCORES) if c != src and topo.host(c) == topo.host(src) and topo.chip(c) == topo.chip(src)
-           and topo.die(c) == topo.die(src) and topo.may_write(c, dst)][0]
-    who = {"H": hlp, "D": dst}
     rank = T.rank_of(core)
-    if rank is None and core != hlp:
+    if rank is None:
         return
     off = topo.mask(src, dst)
-    on = topo.mask(src, hlp) & ~off
-    eng = {"H": on, "D": off}
 
     seen, fin = {}, {}
 
@@ -84,24 +77,36 @@ def rank_program(g, core, T, topo):
         bank["free"][b] = (name, cnt + 2)
         exp(name, 2)
 
-    if rank is not None:
-        g.sync.dma_start(T.wb[:, col(2 * rank)], T.w1[:]).then_inc(T.sem.wl, 16)
-        g.scalar.dma_start(T.wb[:, col(2 * rank + 1)], T.w2[:]).then_inc(T.sem.wl, 16)
-        exp("wl", 32)
+    g.sync.dma_start(T.wb[:, col(2 * rank)], T.w1[:]).then_inc(T.sem.wl, 16)
+    g.scalar.dma_start(T.wb[:, col(2 * rank + 1)], T.w2[:]).then_inc(T.sem.wl, 16)
+    exp("wl", 32)
 
-    if core == src or core == hlp or core == dst:
+    if core == src:
+        qs, i = [g.sync, g.scalar], 0
+        for _, bl in WAVES:
+            for m in bl:
+                qs[i % 2].dma_start(T.h[:, col(m)], T.x[m]).then_inc(T.sem["xl%d" % m], 16)
+                exp("xl%d" % m, 16)
+                i += 1
+
+    if core == src or core == dst:
         g.vector.memset(T.zr[:], 0.0).then_inc(T.sem.zr, 1)
         exp("zr", 1)
+        g.vector.memset(T.one[:], 1.0).then_inc(T.sem.on1, 1)
+        exp("on1", 1)
+        wait(g, "g", "on1", 1)
+        g.affine_select(T.idn[:], T.one[:], [[-1, BK]], AluOpType.is_equal, 0.0, 0, 1).then_inc(T.sem.idn, 1)
+        exp("idn", 1)
 
     def wmask(s):
         m = ~0
-        for d in (hlp, dst):
+        for d in (src, dst):
             if d != cores[s]:
                 m &= topo.mask(cores[s], d)
         return m
 
-    if rank is not None and rank >= 1:
-        ds = [d for d in (hlp, dst) if d != core]
+    if rank >= 1:
+        ds = [d for d in (src, dst) if d != core]
         ap = T.wb[:, col(2 * rank, 2)]
         wait(g, "g", "wl", 32)
         g.remote_dma_fused([RemoteDMATransfer(dst_ids=[did(d) for d in ds], dma_engine_mask=wmask(rank),
@@ -110,43 +115,22 @@ def rank_program(g, core, T, topo):
         exp("ls", _count(wmask(rank)))
 
     if core == src:
-        qs, i = [g.sync, g.scalar], 0
-        for rnd in ROUNDS:
-            for _, ms in rnd:
-                for m in ms:
-                    qs[i % 2].dma_start(T.h[:, col(m)], T.x[m]).then_inc(T.sem["xl%d" % m], 16)
-                    exp("xl%d" % m, 16)
-                    i += 1
-        w = 0
-        for rnd in ROUNDS:
-            ms = [m for _, bl in rnd for m in bl]
+        rid, pid = topo.addr(dst, core)
+        for w, (k, bl) in enumerate(WAVES):
             for sub in range(2):
-                for m in ms:
+                for m in bl:
                     mm("ch%d" % m, 2 * sub, T.wb[:, col(sub)], T.h[:, col(m)], T.h[:, col(m)], sub == 0,
                        [("wl", 32), ("xl%d" % m, 16)])
-            for m in ms:
-                wait(g, "g", "ch%d" % m, 4)
-            trs = []
-            for k, bl in rnd:
+            if k == "D":
+                for m in bl:
+                    wait(g, "g", "ch%d" % m, 4)
                 ap = T.h[:, col(bl[0], len(bl))]
-                trs.append(RemoteDMATransfer(dst_ids=[did(who[k])], dma_engine_mask=eng[k],
-                                             remote_sem=T.sem["ar%d" % w], src=ap, dst=ap))
-                exp("ls", _count(eng[k]))
-                w += 1
-            g.remote_dma_fused(trs, local_sem=T.sem.ls)
+                g.remote_dma(ap, ap, T.sem["ar%d" % w], T.sem.ls, pid, rid, off)
+                exp("ls", _count(off))
 
-    if core == hlp or core == dst:
-        me = "H" if core == hlp else "D"
-        g.vector.memset(T.z[:], 0.0).then_inc(T.sem.idm, 1)
-        wait(g.vector, "v", "idm", 1)
-        g.vector.memset(T.z[:, 0:1], 1.0).then_inc(T.sem.idm, 1)
-        wait(g.sync, "s", "idm", 2)
-        g.sync.dma_start(T.idd[:], T.z[:]).then_inc(T.sem.id1, 16)
-        wait(g.sync, "s", "id1", 16)
-        g.sync.dma_start(T.idn[:], T.idd[0:128, :]).then_inc(T.sem.id2, 16)
-        exp("idm", 2)
-        exp("id1", 16)
-        exp("id2", 16)
+    if core == src or core == dst:
+        me = "S" if core == src else "D"
+        base = 4 if me == "S" else 0
 
         def wdep(s):
             return ("wl", 32) if cores[s] == core else ("wa%d" % s, _count(wmask(s)))
@@ -155,47 +139,42 @@ def rank_program(g, core, T, topo):
             if cores[s] != core:
                 exp("wa%d" % s, _count(wmask(s)))
         for s in range(1, 4):
-            mm("pp%d" % s, 0, T.wb[:, col(2 * s + 1)], T.idn[:], T.wt[:, col(s - 1)], False, [("id2", 16), wdep(s)])
+            mm("pp%d" % s, 0, T.wb[:, col(2 * s + 1)], T.idn[:], T.wt[:, col(s - 1)], False, [("idn", 1), wdep(s)])
         for s in range(1, 4):
             mm("pp%d" % s, 2, T.wt[:, col(s - 1)], T.wb[:, col(2 * s + 2)], T.cs[:, col(s - 1)], False, [wdep(s + 1)])
         lhs = [(T.wb[:, col(2)], wdep(1))] + [(T.cs[:, col(s - 1)], ("pp%d" % s, 4)) for s in range(1, 4)] \
             + [(T.wb[:, col(9)], wdep(4))]
 
-        mine, w = [], 0
-        for rnd in ROUNDS:
-            for k, bl in rnd:
-                if k == me:
-                    mine.append((w, bl))
-                    exp("ar%d" % w, _count(eng[k]))
-                w += 1
-        for gi, grp in enumerate(GROUPS[me]):
-            wm = [(mine[j][0], m) for j in grp for m in mine[j][1]]
+        for w, (k, bl) in enumerate(WAVES):
+            if k != me:
+                continue
+            arr = []
+            if me == "D":
+                arr = [("ar%d" % w, _count(off))]
+                exp("ar%d" % w, _count(off))
             for st in range(5):
-                for wv, m in wm:
-                    mm("ch%d" % m, 2 * st, lhs[st][0], T.h[:, col(m)], T.h[:, col(m)], st < 4,
-                       [lhs[st][1], ("ar%d" % wv, _count(eng[me]))])
-            if me == "H":
-                for _, m in wm:
-                    wait(g, "g", "ch%d" % m, 10)
-                ap = T.h[:, col(wm[0][1], len(wm))]
+                for m in bl:
+                    mm("ch%d" % m, base + 2 * st, lhs[st][0], T.h[:, col(m)], T.h[:, col(m)], st < 4,
+                       [lhs[st][1]] + arr)
+            if me == "S":
+                for m in bl:
+                    wait(g, "g", "ch%d" % m, base + 10)
+                ap = T.h[:, col(bl[0], len(bl))]
                 rid, pid = topo.addr(dst, core)
-                mk = topo.mask(core, dst)
-                g.remote_dma(ap, ap, T.sem["yr%d" % gi], T.sem.ls, pid, rid, mk)
-                exp("ls", _count(mk))
+                g.remote_dma(ap, ap, T.sem.yr0, T.sem.ls, pid, rid, off)
+                exp("ls", _count(off))
             else:
-                for _, m in wm:
+                for m in bl:
                     wait(g.sync, "s", "ch%d" % m, 10)
                     g.sync.dma_start(T.y[m], T.h[:, col(m)]).then_inc(T.sem.st, 16)
                     exp("st", 16)
 
     if core == dst:
-        hw = [bl for rnd in ROUNDS for k, bl in rnd if k == "H"]
-        for gi, grp in enumerate(GROUPS["H"]):
-            n = _count(topo.mask(hlp, dst))
-            exp("yr%d" % gi, n)
-            wait(g.scalar, "a", "yr%d" % gi, n)
-            for j in grp:
-                for m in hw[j]:
+        for k, bl in WAVES:
+            if k == "S":
+                exp("yr0", _count(off))
+                wait(g.scalar, "a", "yr0", _count(off))
+                for m in bl:
                     g.scalar.dma_start(T.y[m], T.h[:, col(m)]).then_inc(T.sem.st, 16)
                     exp("st", 16)
 

@@ -15,7 +15,7 @@ SCRATCH = {
 for _b in range(8):
     SCRATCH["ps%d" % _b] = ("psum", [128, 512], "float32")
 
-SEMAPHORES = (["wl", "zr", "on1", "idn", "ls", "st", "yr0"]
+SEMAPHORES = (["wl", "zr", "on1", "idn", "ls", "st", "yr0", "yr1"]
               + ["wa%d" % s for s in range(1, 5)] + ["pp%d" % s for s in range(1, 4)]
               + ["xl%d" % m for m in range(NB)] + ["ch%d" % m for m in range(NB)]
               + ["ar%d" % w for w in range(3)])
@@ -25,6 +25,10 @@ WAVES = [("D", [0, 1, 2, 3, 4, 5]), ("D", [6, 7, 8, 9]), ("S", [10, 11, 12, 13, 
 
 def _count(mask):
     return sum((mask >> i) & 1 for i in range(32))
+
+
+def _halves(bl):
+    return [bl[:len(bl) // 2], bl[len(bl) // 2:]]
 
 
 def rank_program(g, core, T, topo):
@@ -138,32 +142,57 @@ def rank_program(g, core, T, topo):
         for s in range(1, 5):
             if cores[s] != core:
                 exp("wa%d" % s, _count(wmask(s)))
-        for s in range(1, 4):
+
+        def turn(s):
             mm("pp%d" % s, 0, T.wb[:, col(2 * s + 1)], T.idn[:], T.wt[:, col(s - 1)], False, [("idn", 1), wdep(s)])
-        for s in range(1, 4):
+
+        def fold(s):
             mm("pp%d" % s, 2, T.wt[:, col(s - 1)], T.wb[:, col(2 * s + 2)], T.cs[:, col(s - 1)], False, [wdep(s + 1)])
+
         lhs = [(T.wb[:, col(2)], wdep(1))] + [(T.cs[:, col(s - 1)], ("pp%d" % s, 4)) for s in range(1, 4)] \
             + [(T.wb[:, col(9)], wdep(4))]
 
-        for w, (k, bl) in enumerate(WAVES):
-            if k != me:
-                continue
-            arr = []
-            if me == "D":
-                arr = [("ar%d" % w, _count(off))]
-                exp("ar%d" % w, _count(off))
-            for st in range(5):
-                for m in bl:
-                    mm("ch%d" % m, base + 2 * st, lhs[st][0], T.h[:, col(m)], T.h[:, col(m)], st < 4,
-                       [lhs[st][1]] + arr)
-            if me == "S":
-                for m in bl:
+        def stage(st, bl, arr):
+            for m in bl:
+                mm("ch%d" % m, base + 2 * st, lhs[st][0], T.h[:, col(m)], T.h[:, col(m)], st < 4, [lhs[st][1]] + arr)
+
+        mine = [(w, bl) for w, (k, bl) in enumerate(WAVES) if k == me]
+        for s in range(1, 4):
+            turn(s)
+        if me == "S":
+            bl = mine[0][1]
+            stage(0, _halves(bl)[0], [])
+            fold(1)
+            stage(0, _halves(bl)[1], [])
+            fold(2)
+            fold(3)
+            for st in range(1, 5):
+                stage(st, bl, [])
+            rid, pid = topo.addr(dst, core)
+            for i, part in enumerate(_halves(bl)):
+                for m in part:
                     wait(g, "g", "ch%d" % m, base + 10)
-                ap = T.h[:, col(bl[0], len(bl))]
-                rid, pid = topo.addr(dst, core)
-                g.remote_dma(ap, ap, T.sem.yr0, T.sem.ls, pid, rid, off)
+                ap = T.h[:, col(part[0], len(part))]
+                g.remote_dma(ap, ap, T.sem["yr%d" % i], T.sem.ls, pid, rid, off)
                 exp("ls", _count(off))
-            else:
+        else:
+            for s in range(1, 4):
+                fold(s)
+            for w, bl in mine:
+                exp("ar%d" % w, _count(off))
+            (wa, a), (wb_, b) = mine
+            aa, ab = [("ar%d" % wa, _count(off))], [("ar%d" % wb_, _count(off))]
+            stage(0, a, aa)
+            stage(1, a, aa)
+            stage(0, b, ab)
+            stage(2, a, aa)
+            stage(1, b, ab)
+            stage(3, a, aa)
+            n3 = len(a) // 3
+            for i in range(3):
+                stage(4, a[i * n3:] if i == 2 else a[i * n3:(i + 1) * n3], aa)
+                stage(2 + i, b, ab)
+            for w, bl in mine:
                 for m in bl:
                     wait(g.sync, "s", "ch%d" % m, 10)
                     g.sync.dma_start(T.y[m], T.h[:, col(m)]).then_inc(T.sem.st, 16)
@@ -172,11 +201,12 @@ def rank_program(g, core, T, topo):
     if core == dst:
         for k, bl in WAVES:
             if k == "S":
-                exp("yr0", _count(off))
-                wait(g.scalar, "a", "yr0", _count(off))
-                for m in bl:
-                    g.scalar.dma_start(T.y[m], T.h[:, col(m)]).then_inc(T.sem.st, 16)
-                    exp("st", 16)
+                for i, part in enumerate(_halves(bl)):
+                    exp("yr%d" % i, _count(off))
+                    wait(g.scalar, "a", "yr%d" % i, _count(off))
+                    for m in part:
+                        g.scalar.dma_start(T.y[m], T.h[:, col(m)]).then_inc(T.sem.st, 16)
+                        exp("st", 16)
 
     for name in fin:
         wait(g, "g", name, fin[name])

from concourse.bass import DstId, RemoteDMATransfer
from concourse.mybir import dt, AluOpType

NB, BK = 16, 128

SCRATCH = {
    "h": ("sbuf", [128, NB * BK], "bfloat16"),
    "wb": ("sbuf", [128, 10 * BK], "bfloat16"),
    "wt": ("sbuf", [128, 3 * BK], "bfloat16"),
    "cs": ("sbuf", [128, 3 * BK], "bfloat16"),
    "idn": ("sbuf", [128, BK], "bfloat16"),
    "one": ("sbuf", [128, BK], "bfloat16"),
    "zr": ("sbuf", [128, BK], "float32"),
}
for _b in range(8):
    SCRATCH["ps%d" % _b] = ("psum", [128, 512], "float32")

SEMAPHORES = (["wl", "zr", "on1", "idn", "ls", "st", "yr0", "yr1"]
              + ["wa%d" % s for s in range(1, 5)] + ["pp%d" % s for s in range(1, 4)]
              + ["xl%d" % m for m in range(NB)] + ["ch%d" % m for m in range(NB)]
              + ["ar%d" % w for w in range(3)])

WAVES = [("D", [0, 1, 2, 3, 4, 5]), ("D", [6, 7, 8, 9]), ("S", [10, 11, 12, 13, 14, 15])]


def _count(mask):
    return sum((mask >> i) & 1 for i in range(32))


def _halves(bl):
    return [bl[:len(bl) // 2], bl[len(bl) // 2:]]


def rank_program(g, core, T, topo):
    cores = T.cores
    src, dst = cores[0], cores[-1]
    rank = T.rank_of(core)
    if rank is None:
        return
    off = topo.mask(src, dst)

    seen, fin = {}, {}

    def wait(q, qn, name, val):
        if seen.get((qn, name), 0) >= val:
            return
        seen[(qn, name)] = val
        q.wait_ge(T.sem[name], val)

    def exp(name, n):
        fin[name] = fin.get(name, 0) + n

    def col(m, n=1):
        return slice(m * BK, (m + n) * BK)

    def did(d):
        rid, pid = topo.addr(d, core)
        return DstId(rid=rid, pnc=pid)

    bank = {"i": 0, "free": [None] * 8}

    def mm(name, cnt, lhsT, rhs, out, relu, deps):
        b = bank["i"] % 8
        bank["i"] += 1
        if bank["free"][b] is not None:
            wait(g.tensor, "t", bank["free"][b][0], bank["free"][b][1])
        for d in deps:
            wait(g.tensor, "t", d[0], d[1])
        if cnt:
            wait(g.tensor, "t", name, cnt)
        ps = T["ps%d" % b][:, 0:BK]
        g.tensor.matmul(ps, lhsT, rhs, True, True).then_inc(T.sem[name], 1)
        for d in deps:
            wait(g.vector, "v", d[0], d[1])
        wait(g.vector, "v", name, cnt + 1)
        if relu:
            wait(g.vector, "v", "zr", 1)
            g.vector.tensor_tensor(out, ps, T.zr[:], AluOpType.max).then_inc(T.sem[name], 1)
        else:
            g.vector.tensor_copy(out, ps).then_inc(T.sem[name], 1)
        bank["free"][b] = (name, cnt + 2)
        exp(name, 2)

    g.sync.dma_start(T.wb[:, col(2 * rank)], T.w1[:]).then_inc(T.sem.wl, 16)
    g.scalar.dma_start(T.wb[:, col(2 * rank + 1)], T.w2[:]).then_inc(T.sem.wl, 16)
    exp("wl", 32)

    if core == src:
        qs, i = [g.sync, g.scalar], 0
        for _, bl in WAVES:
            for m in bl:
                qs[i % 2].dma_start(T.h[:, col(m)], T.x[m]).then_inc(T.sem["xl%d" % m], 16)
                exp("xl%d" % m, 16)
                i += 1

    if core == src or core == dst:
        g.vector.memset(T.zr[:], 0.0).then_inc(T.sem.zr, 1)
        exp("zr", 1)
        g.vector.memset(T.one[:], 1.0).then_inc(T.sem.on1, 1)
        exp("on1", 1)
        wait(g, "g", "on1", 1)
        g.affine_select(T.idn[:], T.one[:], [[-1, BK]], AluOpType.is_equal, 0.0, 0, 1).then_inc(T.sem.idn, 1)
        exp("idn", 1)

    def wmask(s):
        m = ~0
        for d in (src, dst):
            if d != cores[s]:
                m &= topo.mask(cores[s], d)
        return m

    if rank >= 1:
        ds = [d for d in (src, dst) if d != core]
        ap = T.wb[:, col(2 * rank, 2)]
        wait(g, "g", "wl", 32)
        g.remote_dma_fused([RemoteDMATransfer(dst_ids=[did(d) for d in ds], dma_engine_mask=wmask(rank),
                                              remote_sem=T.sem["wa%d" % rank], srcs=[ap], dsts=[ap for d in ds])],
                           local_sem=T.sem.ls)
        exp("ls", _count(wmask(rank)))

    if core == src:
        rid, pid = topo.addr(dst, core)
        for w, (k, bl) in enumerate(WAVES):
            for sub in range(2):
                for m in bl:
                    mm("ch%d" % m, 2 * sub, T.wb[:, col(sub)], T.h[:, col(m)], T.h[:, col(m)], sub == 0,
                       [("wl", 32), ("xl%d" % m, 16)])
            if k == "D":
                for m in bl:
                    wait(g, "g", "ch%d" % m, 4)
                ap = T.h[:, col(bl[0], len(bl))]
                g.remote_dma(ap, ap, T.sem["ar%d" % w], T.sem.ls, pid, rid, off)
                exp("ls", _count(off))

    if core == src or core == dst:
        me = "S" if core == src else "D"
        base = 4 if me == "S" else 0

        def wdep(s):
            return ("wl", 32) if cores[s] == core else ("wa%d" % s, _count(wmask(s)))

        for s in range(1, 5):
            if cores[s] != core:
                exp("wa%d" % s, _count(wmask(s)))

        def turn(s):
            mm("pp%d" % s, 0, T.wb[:, col(2 * s + 1)], T.idn[:], T.wt[:, col(s - 1)], False, [("idn", 1), wdep(s)])

        def fold(s):
            mm("pp%d" % s, 2, T.wt[:, col(s - 1)], T.wb[:, col(2 * s + 2)], T.cs[:, col(s - 1)], False, [wdep(s + 1)])

        lhs = [(T.wb[:, col(2)], wdep(1))] + [(T.cs[:, col(s - 1)], ("pp%d" % s, 4)) for s in range(1, 4)] \
            + [(T.wb[:, col(9)], wdep(4))]

        def stage(st, bl, arr):
            for m in bl:
                mm("ch%d" % m, base + 2 * st, lhs[st][0], T.h[:, col(m)], T.h[:, col(m)], st < 4, [lhs[st][1]] + arr)

        mine = [(w, bl) for w, (k, bl) in enumerate(WAVES) if k == me]
        for s in range(1, 4):
            turn(s)
        if me == "S":
            bl = mine[0][1]
            stage(0, _halves(bl)[0], [])
            fold(1)
            stage(0, _halves(bl)[1], [])
            fold(2)
            fold(3)
            for st in range(1, 5):
                stage(st, bl, [])
            rid, pid = topo.addr(dst, core)
            for i, part in enumerate(_halves(bl)):
                for m in part:
                    wait(g, "g", "ch%d" % m, base + 10)
                ap = T.h[:, col(part[0], len(part))]
                g.remote_dma(ap, ap, T.sem["yr%d" % i], T.sem.ls, pid, rid, off)
                exp("ls", _count(off))
        else:
            for s in range(1, 4):
                fold(s)
            for w, bl in mine:
                exp("ar%d" % w, _count(off))
            (wa, a), (wb_, b) = mine
            aa, ab = [("ar%d" % wa, _count(off))], [("ar%d" % wb_, _count(off))]
            stage(0, a, aa)
            stage(1, a, aa)
            stage(0, b, ab)
            stage(2, a, aa)
            stage(1, b, ab)
            stage(3, a, aa)
            n3 = len(a) // 3
            for i in range(3):
                stage(4, a[i * n3:] if i == 2 else a[i * n3:(i + 1) * n3], aa)
                stage(2 + i, b, ab)
            for w, bl in mine:
                for m in bl:
                    wait(g.sync, "s", "ch%d" % m, 10)
                    g.sync.dma_start(T.y[m], T.h[:, col(m)]).then_inc(T.sem.st, 16)
                    exp("st", 16)

    if core == dst:
        for k, bl in WAVES:
            if k == "S":
                for i, part in enumerate(_halves(bl)):
                    exp("yr%d" % i, _count(off))
                    wait(g.scalar, "a", "yr%d" % i, _count(off))
                    for m in part:
                        g.scalar.dma_start(T.y[m], T.h[:, col(m)]).then_inc(T.sem.st, 16)
                        exp("st", 16)

    for name in fin:
        wait(g, "g", name, fin[name])
